import numpy as np
import ml_dtypes


def mxq(x, axis, fmt="e4m3"):
    dtype, down = {"e4m3": (ml_dtypes.float8_e4m3fn, 7), "e5m2": (ml_dtypes.float8_e5m2, 14)}[fmt]
    v = np.moveaxis(np.asarray(x, np.float32).astype(ml_dtypes.bfloat16).astype(np.float64), axis, -1)
    blocks = v.reshape(v.shape[:-1] + (-1, 32))
    amax = np.abs(blocks).max(-1, keepdims=True)
    byte = np.maximum(np.where(amax > 0, np.frexp(amax)[1] - 1 + 127, 0) - down, 1)
    scale = np.exp2(byte - 127.0)
    codes = (blocks / scale).astype(np.float32).astype(dtype).astype(np.float64)
    return np.moveaxis((codes * scale).reshape(v.shape), -1, axis)


WIDE = False


def mx_kscale(k):
    if not WIDE:
        return np.ones(k)
    levels = np.array([10, -10, 5, -5, 0])
    if k % 512:
        return np.exp2(np.random.permutation(np.resize(levels, k // 32))).repeat(32)
    a = np.empty((k // 512, 16))
    for p in range(k // 512):
        a[p, :8] = np.random.permutation(np.resize(levels, 8))
        for g in range(8):
            far = levels[np.abs(levels - a[p, g]) >= 10]
            a[p, g + 8] = far[np.random.randint(len(far))]
    return np.exp2(a.ravel()).repeat(32)


def f64(x):
    return np.asarray(x).astype(np.float64)


def striped(idx):
    return np.tile(idx.reshape(-1, 16).T, (8, 1)).astype(np.uint16)


def unstriped(offs):
    return offs[:16].T.reshape(-1).astype(np.int64)


def striped8(idx):
    return np.concatenate([x.reshape(-1, 16).T for x in idx]).astype(np.uint16)


def runs(offs, k):
    lists = np.stack([offs[16 * r : 16 * r + 16].T.reshape(-1) for r in range(8)]).astype(np.int64)
    return lists[np.arange(k) % 512 // 64]


def pack_weight(w):
    k, n = w.shape
    w = f64(np.asarray(w, np.float32).astype(ml_dtypes.bfloat16)).reshape(k // 32, 32, n)
    amax = np.abs(w).max(1)
    byte = np.clip(np.where(amax > 0, np.frexp(amax)[1] - 1 + 127 - 7, 1), 1, 254)
    scaled = (w * np.exp2(127.0 - byte)[:, None, :]).reshape(k, n).astype(np.float32)
    words = np.ascontiguousarray(scaled.reshape(k // 512, 128, 4, n).transpose(0, 1, 3, 2)).astype(ml_dtypes.float8_e4m3fn).view(np.uint8)
    return words, np.ascontiguousarray(byte.astype(np.uint8).reshape(k // 512, 16, n))


def unpack_weight(words, scales):
    g, p, n, _ = words.shape
    vals = np.ascontiguousarray(words).view(ml_dtypes.float8_e4m3fn).astype(np.float64) * np.repeat(np.exp2(scales.astype(np.float64) - 127.0), 8, axis=1)[..., None]
    return vals.transpose(0, 1, 3, 2).reshape(g * 512, n)

def planes(y):
    n, m = y.shape
    v = y.astype(np.float32).astype(ml_dtypes.bfloat16).astype(np.float64).reshape(n // 32, 32, m)
    top = np.abs(v).max(1)
    byte = np.clip(np.where(top > 0, np.frexp(top)[1] - 1 + 127 - 7, 1), 1, 254)
    codes = (v * np.exp2(127.0 - byte)[:, None, :]).reshape(n, m).astype(np.float32).astype(ml_dtypes.float8_e4m3fn).view(np.uint8)
    words = codes.reshape(n // 512, 128, 4, m).transpose(0, 1, 3, 2)
    return np.ascontiguousarray(words), np.ascontiguousarray(byte.astype(np.uint8).reshape(n // 512, 16, m))


K, T, S, G, H, C = 512, 1024, 512, 2048, 512, 512


def setup_inputs():
    n = np.random.standard_normal
    s = mx_kscale(K)[:, None]
    packed_xT = pack_weight(n((K, T)) * s)
    packed_dT = pack_weight(n((K, G)) / s)
    return {
        "x_words": packed_xT[0],
        "x_scales": packed_xT[1],
        "d_words": packed_dT[0],
        "d_scales": packed_dT[1],
        "gs": (np.random.uniform(0.5, 1.5, (K, 1)) / s).astype(np.float32),
        "offs": striped(np.random.permutation(T)[:S]),
        "k1": striped8(np.random.randint(0, G, (8, H))),
        "n1": striped8(np.stack([np.random.permutation(S) for _ in range(8)])),
        "n2": striped8(np.stack([np.random.permutation(S) for _ in range(8)])),
        "n3": striped8(np.stack([np.random.permutation(S) for _ in range(8)])),
        "cand": striped(np.random.permutation(T)[:C]),
        "n4": striped8(np.stack([np.random.permutation(S) for _ in range(8)])),
        "n5": striped8(np.stack([np.random.permutation(S) for _ in range(8)])),
    }


def reference(x_words, x_scales, d_words, d_scales, gs, offs, k1, n1, n2, n3, cand, n4, n5):
    x_cand = unpack_weight(x_words, x_scales)[:, unstriped(cand)]
    d_k1 = unpack_weight(d_words, d_scales)[np.arange(K)[:, None], runs(k1, K)]
    xq = unpack_weight(x_words, x_scales)[:, unstriped(offs)]
    h = 0.0625 * (d_k1.T @ xq)
    z = f64(gs) * (0.75 * (h * (h[np.arange(H)[:, None], runs(n1, H)]) + (h[np.arange(H)[:, None], runs(n2, H)]) * (h[np.arange(H)[:, None], runs(n3, H)])))
    s = 0.0625 * ((x_cand.T @ mxq(z, 0, "e4m3")))
    out_0 = np.maximum(s[np.arange(C)[:, None], runs(n4, C)], s[np.arange(C)[:, None], runs(n5, C)]) - (0.75 * s)
    return (out_0,) + planes(out_0)

@@ -1,0 +1,192 @@
+from contextlib import ExitStack
+
+import concourse.mybir as mybir
+
+K, T, S, G = 512, 1024, 512, 2048
+FLOPS = 2 * 2 * 512 * 512 * 512
+
+F32 = mybir.dt.float32
+BF16 = mybir.dt.bfloat16
+I32 = mybir.dt.int32
+U32 = mybir.dt.uint32
+U16 = mybir.dt.uint16
+U8 = mybir.dt.uint8
+FP8X4 = mybir.dt.float8_e4m3fn_x4
+ALU = mybir.AluOpType
+COPY = mybir.ActivationFunctionType.Copy
+
+P = 128
+PACK = 4
+CHUNKS = ((0, 256), (256, 384), (384, 512))
+
+
+def tile_picked_pqcdotover_none_po_kernel(
+    tc, x_words, x_scales, d_words, d_scales, gs, offs, k1, n1, n2, n3, cand, n4, n5, out_0, out_1, out_2
+):
+    nc = tc.nc
+    with ExitStack() as ctx:
+        keep = ctx.enter_context(tc.tile_pool(name="keep", bufs=1))
+        psum = ctx.enter_context(tc.psum_pool(name="psum", bufs=1))
+
+        def sb(name, shape, dtype):
+            return keep.tile(shape, dtype, name=name, align_bytes=64)
+
+        def load_list(name, src):
+            tile = sb(name, [P, S // 16], U16)
+            nc.sync.dma_start(tile[:], src)
+            return tile
+
+        def word_rows(words):
+            return words[0].rearrange("p c r -> p (c r)").bitcast(I32)
+
+        d_byte_table = sb("d_byte_table", [P, G], U8)
+        x_byte_table = sb("x_byte_table", [P, T], U8)
+        d_plane = sb("d_plane", [P, S], U8)
+        nc.vector.memset(d_byte_table[:].bitcast(I32), 0)
+        nc.gpsimd.memset(x_byte_table[:].bitcast(I32), 0)
+        nc.vector.memset(d_plane[:].bitcast(I32), 0)
+
+        k1_t = load_list("k1_t", k1)
+        nc.scalar.dma_start(d_byte_table[0:P:8, :].bitcast(I32), d_scales[0].bitcast(I32))
+        d_word_table = sb("d_word_table", [P, G], U32)
+        nc.sync.dma_start(d_word_table[:].bitcast(I32), word_rows(d_words))
+        offs_t = load_list("offs_t", offs)
+        x_word_table = sb("x_word_table", [P, T], U32)
+        nc.sync.dma_start(x_word_table[:].bitcast(I32), word_rows(x_words))
+        for q in range(4):
+            nc.gpsimd.dma_start(
+                x_byte_table[32 * q : 32 * q + 4, :].bitcast(I32), x_scales[0][4 * q : 4 * q + 4, :].bitcast(I32)
+            )
+        cand_t = load_list("cand_t", cand)
+        gs_t = sb("gs_t", [P, PACK], F32)
+        nc.gpsimd.dma_start(gs_t[:], gs.rearrange("(p t) o -> p (t o)", t=PACK))
+        n2_t = load_list("n2_t", n2)
+        n1_t = load_list("n1_t", n1)
+        n3_t = load_list("n3_t", n3)
+        n4_t = load_list("n4_t", n4)
+        n5_t = load_list("n5_t", n5)
+
+        def pick(name, table, entries, dtype):
+            picked = sb(name, [P, S], dtype)
+            nc.vector.tensor_copy(picked[:], table[:].indirect(entries[:]))
+            return picked
+
+        def deal(name, picked, dtype):
+            dealt = sb(name, [P, S], dtype)
+            nc.vector.tensor_copy(
+                dealt[:].rearrange("p (t m) -> p m t", t=PACK), picked[:].rearrange("p (m t) -> p m t", t=PACK)
+            )
+            return dealt
+
+        d_bytes = deal("d_bytes", pick("d_bytes_picked", d_byte_table, k1_t, U8), U8)
+        for q in range(4):
+            nc.scalar.dma_start(
+                d_plane[32 * q : 32 * q + 4, :].bitcast(I32), d_bytes[32 * q : 32 * q + 32 : 8, :].bitcast(I32)
+            )
+        d_codes = deal("d_codes", pick("d_codes_picked", d_word_table, k1_t, U32), U32)
+        x_codes = pick("x_codes", x_word_table, offs_t, U32)
+        x_plane = pick("x_plane", x_byte_table, offs_t, U8)
+
+        h_plain, h_gated = [], []
+        for t in range(PACK):
+            rows = slice(P * t, P * (t + 1))
+            bank = psum.tile([P, S], F32, name="h_bank%d" % t, tag="bank%d" % t)
+            nc.tensor.matmul_mx(
+                out=bank[:],
+                lhsT=d_codes[:, rows].bitcast(FP8X4),
+                lhsT_scale=d_plane[:, rows],
+                rhs=x_codes[:].bitcast(FP8X4),
+                rhs_scale=x_plane[:],
+                start=True,
+                stop=True,
+            )
+            gated = sb("h_gated%d" % t, [P, S], F32)
+            nc.scalar.activation(gated[:], bank[:], COPY, scale=gs_t[:, t : t + 1])
+            plain = sb("h_plain%d" % t, [P, S], F32)
+            nc.scalar.activation(plain[:], bank[:], COPY, scale=0.75 * 0.0625 * 0.0625)
+            h_plain.append(plain)
+            h_gated.append(gated)
+
+        c_plane = deal("c_plane", pick("c_bytes_picked", x_byte_table, cand_t, U8), U8)
+        c_codes = deal("c_codes", pick("c_codes_picked", x_word_table, cand_t, U32), U32)
+
+        s_win = [sb("s_win%d" % t, [P, S], F32) for t in range(PACK)]
+        s_own = []
+        for c, (lo, hi) in enumerate(CHUNKS):
+            n = hi - lo
+            cols = slice(lo, hi)
+            ent = slice(lo // 16, hi // 16)
+            second = sb("second%d" % c, [P, PACK, n], F32)
+            first_prod = sb("first_prod%d" % c, [P, PACK, n], F32)
+            second_prod = sb("second_prod%d" % c, [P, PACK, n], F32)
+            for t in range(PACK):
+                nc.vector.tensor_copy(second[:, t, :], h_gated[t][:].indirect(n2_t[:, ent]))
+                nc.vector.tensor_tensor(
+                    first_prod[:, t, :], h_plain[t][:].indirect(n1_t[:, ent]), h_gated[t][:, cols], ALU.mult
+                )
+                nc.vector.tensor_tensor(
+                    second_prod[:, t, :], h_plain[t][:].indirect(n3_t[:, ent]), second[:, t, :], ALU.mult
+                )
+            z = sb("z%d" % c, [P, n, PACK], BF16)
+            nc.vector.tensor_tensor(
+                z[:].rearrange("p (c i) t -> p c t i", i=4),
+                first_prod[:].rearrange("p t (c i) -> p c t i", i=4),
+                second_prod[:].rearrange("p t (c i) -> p c t i", i=4),
+                ALU.add,
+            )
+            z_codes = sb("z_codes%d" % c, [P, n], U32)
+            z_plane = sb("z_plane%d" % c, [P, n], U8)
+            nc.vector.quantize_mx(
+                out=z_codes[:].bitcast(FP8X4), scales=z_plane[:], in_=z[:].rearrange("p c t -> p (c t)")
+            )
+            own = sb("s_own%d" % c, [P, PACK, n], F32)
+            s_own.append(own)
+            for t in range(PACK):
+                rows = slice(P * t, P * (t + 1))
+                tag = "bank%d" % (t + PACK * ((c + 1) % 2))
+                bank = psum.tile([P, n], F32, name="s_bank%d_%d" % (c, t), tag=tag)
+                nc.tensor.matmul_mx(
+                    out=bank[:],
+                    lhsT=c_codes[:, rows].bitcast(FP8X4),
+                    lhsT_scale=c_plane[:, rows],
+                    rhs=z_codes[:].bitcast(FP8X4),
+                    rhs_scale=z_plane[:],
+                    start=True,
+                    stop=True,
+                )
+                nc.scalar.activation(s_win[t][:, cols], bank[:], COPY, scale=0.0625)
+                nc.scalar.activation(own[:, t, :], bank[:], COPY, scale=0.75 * 0.0625)
+
+        out_rows = out_0.rearrange("(p t) j -> p t j", t=PACK)
+        out_words = word_rows(out_1)
+        y_plane = sb("y_plane", [P, S], U8)
+        for c, (lo, hi) in enumerate(CHUNKS):
+            n = hi - lo
+            cols = slice(lo, hi)
+            ent = slice(lo // 16, hi // 16)
+            left = sb("left%d" % c, [P, PACK, n], F32)
+            right = sb("right%d" % c, [P, PACK, n], F32)
+            for t in range(PACK):
+                nc.vector.tensor_tensor(
+                    left[:, t, :], s_win[t][:].indirect(n4_t[:, ent]), s_own[c][:, t, :], ALU.subtract
+                )
+                nc.vector.tensor_tensor(
+                    right[:, t, :], s_win[t][:].indirect(n5_t[:, ent]), s_own[c][:, t, :], ALU.subtract
+                )
+            y = sb("y%d" % c, [P, PACK, n], F32)
+            nc.vector.tensor_tensor(y[:], left[:], right[:], ALU.max)
+            nc.sync.dma_start(out_rows[:, :, cols], y[:])
+            y_round = sb("y_round%d" % c, [P, n, PACK], BF16)
+            nc.scalar.copy(
+                y_round[:].rearrange("p (c i) t -> p c t i", i=4), y[:].rearrange("p t (c i) -> p c t i", i=4)
+            )
+            y_codes = sb("y_codes%d" % c, [P, n], U32)
+            nc.vector.quantize_mx(
+                out=y_codes[:].bitcast(FP8X4), scales=y_plane[:, cols], in_=y_round[:].rearrange("p c t -> p (c t)")
+            )
+            nc.sync.dma_start(out_words[:, cols], y_codes[:].bitcast(I32))
+        for q in range(4):
+            queue = nc.sync if q % 2 else nc.scalar
+            queue.dma_start(
+                out_2[0][4 * q : 4 * q + 4, :].bitcast(I32), y_plane[32 * q : 32 * q + 4, :].bitcast(I32)
+            )

@@ -1,6 +1,7 @@
 from contextlib import ExitStack
 
 import concourse.mybir as mybir
+from concourse.masks import make_identity
 
 K, T, S, G = 512, 1024, 512, 2048
 FLOPS = 2 * 2 * 512 * 512 * 512
@@ -28,8 +29,8 @@ def tile_picked_pqcdotover_none_po_kernel(
         keep = ctx.enter_context(tc.tile_pool(name="keep", bufs=1))
         psum = ctx.enter_context(tc.psum_pool(name="psum", bufs=1))
 
-        def sb(name, shape, dtype):
-            return keep.tile(shape, dtype, name=name, align_bytes=64)
+        def sb(name, shape, dtype, tag=None):
+            return keep.tile(shape, dtype, name=name, tag=tag or name, align_bytes=64)
 
         def load_list(name, src):
             tile = sb(name, [P, S // 16], U16)
@@ -42,50 +43,61 @@ def tile_picked_pqcdotover_none_po_kernel(
         d_byte_table = sb("d_byte_table", [P, G], U8)
         x_byte_table = sb("x_byte_table", [P, T], U8)
         d_plane = sb("d_plane", [P, S], U8)
-        nc.vector.memset(d_byte_table[:].bitcast(I32), 0)
-        nc.gpsimd.memset(x_byte_table[:].bitcast(I32), 0)
+        nc.gpsimd.memset(d_byte_table[:].bitcast(I32), 0)
+        nc.vector.memset(x_byte_table[:].bitcast(I32), 0)
         nc.vector.memset(d_plane[:].bitcast(I32), 0)
+        identity = sb("identity", [P, P], F32)
+        make_identity(nc, identity[:])
 
-        k1_t = load_list("k1_t", k1)
-        nc.scalar.dma_start(d_byte_table[0:P:8, :].bitcast(I32), d_scales[0].bitcast(I32))
-        d_word_table = sb("d_word_table", [P, G], U32)
-        nc.sync.dma_start(d_word_table[:].bitcast(I32), word_rows(d_words))
         offs_t = load_list("offs_t", offs)
+        k1_t = load_list("k1_t", k1)
         x_word_table = sb("x_word_table", [P, T], U32)
         nc.sync.dma_start(x_word_table[:].bitcast(I32), word_rows(x_words))
+        nc.sync.dma_start(d_byte_table[0:P:8, :].bitcast(I32), d_scales[0].bitcast(I32))
+        cand_t = load_list("cand_t", cand)
         for q in range(4):
-            nc.gpsimd.dma_start(
+            nc.scalar.dma_start(
                 x_byte_table[32 * q : 32 * q + 4, :].bitcast(I32), x_scales[0][4 * q : 4 * q + 4, :].bitcast(I32)
             )
-        cand_t = load_list("cand_t", cand)
         gs_t = sb("gs_t", [P, PACK], F32)
-        nc.gpsimd.dma_start(gs_t[:], gs.rearrange("(p t) o -> p (t o)", t=PACK))
+        nc.scalar.dma_start(gs_t[:], gs.rearrange("(p t) o -> p (t o)", t=PACK))
         n2_t = load_list("n2_t", n2)
         n1_t = load_list("n1_t", n1)
         n3_t = load_list("n3_t", n3)
         n4_t = load_list("n4_t", n4)
         n5_t = load_list("n5_t", n5)
+        d_word_table = sb("d_word_table", [P, G], U32)
+        nc.sync.dma_start(d_word_table[:].bitcast(I32), word_rows(d_words))
 
-        def pick(name, table, entries, dtype):
-            picked = sb(name, [P, S], dtype)
+        def pick(name, table, entries, dtype, tag=None):
+            picked = sb(name, [P, S], dtype, tag)
             nc.vector.tensor_copy(picked[:], table[:].indirect(entries[:]))
             return picked
 
-        def deal(name, picked, dtype):
-            dealt = sb(name, [P, S], dtype)
+        def deal_words(name, picked):
+            dealt = sb(name, [P, S], U32)
             nc.vector.tensor_copy(
-                dealt[:].rearrange("p (t m) -> p m t", t=PACK), picked[:].rearrange("p (m t) -> p m t", t=PACK)
+                dealt[:].rearrange("p (t c i) -> p c t i", t=PACK, i=4),
+                picked[:].rearrange("p (c i t) -> p c t i", t=PACK, i=4),
             )
             return dealt
 
-        d_bytes = deal("d_bytes", pick("d_bytes_picked", d_byte_table, k1_t, U8), U8)
+        def deal_bytes(name, picked):
+            dealt = sb(name, [P, S], U8)
+            nc.vector.tensor_copy(
+                dealt[:].rearrange("p (t m) -> p t m", t=PACK), picked[:].rearrange("p (m t) -> p t m", t=PACK)
+            )
+            return dealt
+
+        x_codes = pick("x_codes", x_word_table, offs_t, U32)
+        d_bytes = deal_bytes("d_bytes", pick("d_bytes_picked", d_byte_table, k1_t, U8, "staging"))
         for q in range(4):
             nc.scalar.dma_start(
                 d_plane[32 * q : 32 * q + 4, :].bitcast(I32), d_bytes[32 * q : 32 * q + 32 : 8, :].bitcast(I32)
             )
-        d_codes = deal("d_codes", pick("d_codes_picked", d_word_table, k1_t, U32), U32)
-        x_codes = pick("x_codes", x_word_table, offs_t, U32)
+        c_codes = deal_words("c_codes", pick("c_codes_picked", x_word_table, cand_t, U32))
         x_plane = pick("x_plane", x_byte_table, offs_t, U8)
+        d_codes = deal_words("d_codes", pick("d_codes_picked", d_word_table, k1_t, U32, "staging"))
 
         h_plain, h_gated = [], []
         for t in range(PACK):
@@ -107,18 +119,24 @@ def tile_picked_pqcdotover_none_po_kernel(
             h_plain.append(plain)
             h_gated.append(gated)
 
-        c_plane = deal("c_plane", pick("c_bytes_picked", x_byte_table, cand_t, U8), U8)
-        c_codes = deal("c_codes", pick("c_codes_picked", x_word_table, cand_t, U32), U32)
+        c_plane = deal_bytes("c_plane", pick("c_bytes_picked", x_byte_table, cand_t, U8, "staging"))
 
         s_win = [sb("s_win%d" % t, [P, S], F32) for t in range(PACK)]
         s_own = []
+        last = len(CHUNKS) - 1
         for c, (lo, hi) in enumerate(CHUNKS):
             n = hi - lo
             cols = slice(lo, hi)
             ent = slice(lo // 16, hi // 16)
-            second = sb("second%d" % c, [P, PACK, n], F32)
+            blocks = range(n // P)
+            second = sb("second%d" % c, [P, PACK, n], F32, "z0" if c == last else None)
             first_prod = sb("first_prod%d" % c, [P, PACK, n], F32)
             second_prod = sb("second_prod%d" % c, [P, PACK, n], F32)
+            if c < last:
+                sums = [
+                    psum.tile([P, PACK, P], F32, name="sum%d_%d" % (c, b), tag="bank%d" % (4 + c + b))
+                    for b in blocks
+                ]
             for t in range(PACK):
                 nc.vector.tensor_copy(second[:, t, :], h_gated[t][:].indirect(n2_t[:, ent]))
                 nc.vector.tensor_tensor(
@@ -127,26 +145,56 @@ def tile_picked_pqcdotover_none_po_kernel(
                 nc.vector.tensor_tensor(
                     second_prod[:, t, :], h_plain[t][:].indirect(n3_t[:, ent]), second[:, t, :], ALU.mult
                 )
-            z = sb("z%d" % c, [P, n, PACK], BF16)
-            nc.vector.tensor_tensor(
-                z[:].rearrange("p (c i) t -> p c t i", i=4),
-                first_prod[:].rearrange("p t (c i) -> p c t i", i=4),
-                second_prod[:].rearrange("p t (c i) -> p c t i", i=4),
-                ALU.add,
-            )
+                if c < last:
+                    for b in blocks:
+                        for term, opens in ((first_prod, True), (second_prod, False)):
+                            nc.tensor.matmul(
+                                sums[b][:, t, :],
+                                term[:, t, P * b : P * (b + 1)],
+                                identity[:],
+                                start=opens,
+                                stop=not opens,
+                                is_transpose=True,
+                            )
+            z = sb("z%d" % c, [P, n * PACK], BF16, "z%d" % min(c, 1))
+            if c < last:
+                back = psum.tile([P, n // P, 2, P], F32, name="back%d" % c, tag="bank7")
+                for b in blocks:
+                    turned = sb("turned%d_%d" % (c, b), [P, PACK * P], BF16)
+                    nc.scalar.copy(
+                        turned[:].rearrange("j (u p e) -> j u p e", u=2, e=2),
+                        sums[b][:].rearrange("j (u e) p -> j u p e", u=2),
+                    )
+                    for u in range(2):
+                        nc.tensor.transpose(
+                            back[:, b, u, :], turned[:].bitcast(F32)[:, P * u : P * (u + 1)], identity[:]
+                        )
+                nc.scalar.copy(
+                    z[:].bitcast(F32).rearrange("p (b j u) -> p b j u", j=P, u=2),
+                    back[:].rearrange("p b u j -> p b j u"),
+                )
+            else:
+                nc.vector.tensor_tensor(
+                    z[:].rearrange("p (c t) -> p c t", t=PACK),
+                    first_prod[:].rearrange("p t c -> p c t"),
+                    second_prod[:].rearrange("p t c -> p c t"),
+                    ALU.add,
+                )
             z_codes = sb("z_codes%d" % c, [P, n], U32)
             z_plane = sb("z_plane%d" % c, [P, n], U8)
-            nc.vector.quantize_mx(
-                out=z_codes[:].bitcast(FP8X4), scales=z_plane[:], in_=z[:].rearrange("p c t -> p (c t)")
-            )
+            nc.vector.quantize_mx(out=z_codes[:].bitcast(FP8X4), scales=z_plane[:], in_=z[:])
             own = sb("s_own%d" % c, [P, PACK, n], F32)
             s_own.append(own)
+            per_bank = 1 if c == last else S // n
+            first_bank = (0, 2, 3)[c]
+            banks = [
+                psum.tile([P, per_bank, n], F32, name="s_bank%d_%d" % (c, g), tag="bank%d" % (first_bank + g))
+                for g in range(PACK // per_bank)
+            ]
             for t in range(PACK):
                 rows = slice(P * t, P * (t + 1))
-                tag = "bank%d" % (t + PACK * ((c + 1) % 2))
-                bank = psum.tile([P, n], F32, name="s_bank%d_%d" % (c, t), tag=tag)
                 nc.tensor.matmul_mx(
-                    out=bank[:],
+                    out=banks[t // per_bank][:, t % per_bank, :],
                     lhsT=c_codes[:, rows].bitcast(FP8X4),
                     lhsT_scale=c_plane[:, rows],
                     rhs=z_codes[:].bitcast(FP8X4),
@@ -154,8 +202,12 @@ def tile_picked_pqcdotover_none_po_kernel(
                     start=True,
                     stop=True,
                 )
-                nc.scalar.activation(s_win[t][:, cols], bank[:], COPY, scale=0.0625)
-                nc.scalar.activation(own[:, t, :], bank[:], COPY, scale=0.75 * 0.0625)
+            for t in range(PACK):
+                nc.scalar.activation(s_win[t][:, cols], banks[t // per_bank][:, t % per_bank, :], COPY, scale=0.0625)
+            for g, bank in enumerate(banks):
+                nc.scalar.activation(
+                    own[:, per_bank * g : per_bank * (g + 1), :], bank[:], COPY, scale=0.75 * 0.0625
+                )
 
         out_rows = out_0.rearrange("(p t) j -> p t j", t=PACK)
         out_words = word_rows(out_1)
@@ -177,7 +229,8 @@ def tile_picked_pqcdotover_none_po_kernel(
             nc.vector.tensor_tensor(y[:], left[:], right[:], ALU.max)
             nc.sync.dma_start(out_rows[:, :, cols], y[:])
             y_round = sb("y_round%d" % c, [P, n, PACK], BF16)
-            nc.scalar.copy(
+            regroup = nc.vector.tensor_copy if c == last else nc.scalar.copy
+            regroup(
                 y_round[:].rearrange("p (c i) t -> p c t i", i=4), y[:].rearrange("p t (c i) -> p c t i", i=4)
             )
             y_codes = sb("y_codes%d" % c, [P, n], U32)

@@ -49,25 +49,25 @@ def tile_picked_pqcdotover_none_po_kernel(
         identity = sb("identity", [P, P], F32)
         make_identity(nc, identity[:])
 
-        offs_t = load_list("offs_t", offs)
-        k1_t = load_list("k1_t", k1)
         x_word_table = sb("x_word_table", [P, T], U32)
         nc.sync.dma_start(x_word_table[:].bitcast(I32), word_rows(x_words))
+        offs_t = load_list("offs_t", offs)
+        k1_t = load_list("k1_t", k1)
         nc.sync.dma_start(d_byte_table[0:P:8, :].bitcast(I32), d_scales[0].bitcast(I32))
         cand_t = load_list("cand_t", cand)
+        n2_t = load_list("n2_t", n2)
+        n1_t = load_list("n1_t", n1)
+        d_word_table = sb("d_word_table", [P, G], U32)
+        nc.sync.dma_start(d_word_table[:].bitcast(I32), word_rows(d_words))
         for q in range(4):
             nc.scalar.dma_start(
                 x_byte_table[32 * q : 32 * q + 4, :].bitcast(I32), x_scales[0][4 * q : 4 * q + 4, :].bitcast(I32)
             )
         gs_t = sb("gs_t", [P, PACK], F32)
-        nc.scalar.dma_start(gs_t[:], gs.rearrange("(p t) o -> p (t o)", t=PACK))
-        n2_t = load_list("n2_t", n2)
-        n1_t = load_list("n1_t", n1)
+        nc.gpsimd.dma_start(gs_t[:], gs.rearrange("(p t) o -> p (t o)", t=PACK))
         n3_t = load_list("n3_t", n3)
         n4_t = load_list("n4_t", n4)
         n5_t = load_list("n5_t", n5)
-        d_word_table = sb("d_word_table", [P, G], U32)
-        nc.sync.dma_start(d_word_table[:].bitcast(I32), word_rows(d_words))
 
         def pick(name, table, entries, dtype, tag=None):
             picked = sb(name, [P, S], dtype, tag)
@@ -95,9 +95,8 @@ def tile_picked_pqcdotover_none_po_kernel(
             nc.scalar.dma_start(
                 d_plane[32 * q : 32 * q + 4, :].bitcast(I32), d_bytes[32 * q : 32 * q + 32 : 8, :].bitcast(I32)
             )
-        c_codes = deal_words("c_codes", pick("c_codes_picked", x_word_table, cand_t, U32))
-        x_plane = pick("x_plane", x_byte_table, offs_t, U8)
         d_codes = deal_words("d_codes", pick("d_codes_picked", d_word_table, k1_t, U32, "staging"))
+        x_plane = pick("x_plane", x_byte_table, offs_t, U8)
 
         h_plain, h_gated = [], []
         for t in range(PACK):
@@ -119,77 +118,102 @@ def tile_picked_pqcdotover_none_po_kernel(
             h_plain.append(plain)
             h_gated.append(gated)
 
-        c_plane = deal_bytes("c_plane", pick("c_bytes_picked", x_byte_table, cand_t, U8, "staging"))
+        c_codes_picked = pick("c_codes_picked", x_word_table, cand_t, U32, "staging")
+        c_bytes_picked = pick("c_bytes_picked", x_byte_table, cand_t, U8, "d_word_table")
+        c_codes = deal_words("c_codes", c_codes_picked)
+        c_plane = deal_bytes("c_plane", c_bytes_picked)
 
         s_win = [sb("s_win%d" % t, [P, S], F32) for t in range(PACK)]
-        s_own = []
+        s_own = [sb("s_own%d" % c, [P, PACK, hi - lo], F32) for c, (lo, hi) in enumerate(CHUNKS)]
         last = len(CHUNKS) - 1
-        for c, (lo, hi) in enumerate(CHUNKS):
+
+        def products(c):
+            lo, hi = CHUNKS[c]
             n = hi - lo
-            cols = slice(lo, hi)
             ent = slice(lo // 16, hi // 16)
-            blocks = range(n // P)
-            second = sb("second%d" % c, [P, PACK, n], F32, "z0" if c == last else None)
-            first_prod = sb("first_prod%d" % c, [P, PACK, n], F32)
+            second = sb("second%d" % c, [P, PACK, n], F32, "z0" if c == last else "second")
+            first_prod = sb("first_prod", [P, PACK, n], F32) if c == 0 else second
             second_prod = sb("second_prod%d" % c, [P, PACK, n], F32)
-            if c < last:
-                sums = [
-                    psum.tile([P, PACK, P], F32, name="sum%d_%d" % (c, b), tag="bank%d" % (4 + c + b))
-                    for b in blocks
-                ]
-            for t in range(PACK):
+
+            def fetch_second(t):
                 nc.vector.tensor_copy(second[:, t, :], h_gated[t][:].indirect(n2_t[:, ent]))
+
+            def multiply_first(t):
                 nc.vector.tensor_tensor(
-                    first_prod[:, t, :], h_plain[t][:].indirect(n1_t[:, ent]), h_gated[t][:, cols], ALU.mult
+                    first_prod[:, t, :], h_plain[t][:].indirect(n1_t[:, ent]), h_gated[t][:, lo:hi], ALU.mult
                 )
+
+            def multiply_second(t):
                 nc.vector.tensor_tensor(
                     second_prod[:, t, :], h_plain[t][:].indirect(n3_t[:, ent]), second[:, t, :], ALU.mult
                 )
-                if c < last:
-                    for b in blocks:
-                        for term, opens in ((first_prod, True), (second_prod, False)):
-                            nc.tensor.matmul(
-                                sums[b][:, t, :],
-                                term[:, t, P * b : P * (b + 1)],
-                                identity[:],
-                                start=opens,
-                                stop=not opens,
-                                is_transpose=True,
-                            )
-            z = sb("z%d" % c, [P, n * PACK], BF16, "z%d" % min(c, 1))
-            if c < last:
-                back = psum.tile([P, n // P, 2, P], F32, name="back%d" % c, tag="bank7")
-                for b in blocks:
-                    turned = sb("turned%d_%d" % (c, b), [P, PACK * P], BF16)
-                    nc.scalar.copy(
-                        turned[:].rearrange("j (u p e) -> j u p e", u=2, e=2),
-                        sums[b][:].rearrange("j (u e) p -> j u p e", u=2),
-                    )
-                    for u in range(2):
-                        nc.tensor.transpose(
-                            back[:, b, u, :], turned[:].bitcast(F32)[:, P * u : P * (u + 1)], identity[:]
-                        )
-                nc.scalar.copy(
-                    z[:].bitcast(F32).rearrange("p (b j u) -> p b j u", j=P, u=2),
-                    back[:].rearrange("p b u j -> p b j u"),
-                )
+
+            if c == 0:
+                for t in range(PACK):
+                    for step in (fetch_second, multiply_first, multiply_second):
+                        step(t)
             else:
-                nc.vector.tensor_tensor(
-                    z[:].rearrange("p (c t) -> p c t", t=PACK),
-                    first_prod[:].rearrange("p t c -> p c t"),
-                    second_prod[:].rearrange("p t c -> p c t"),
-                    ALU.add,
+                for step in (fetch_second, multiply_second, multiply_first):
+                    for t in range(PACK):
+                        step(t)
+            return (first_prod, second_prod) if c == 0 else (second_prod, first_prod)
+
+        def sum_on_tensor(c, terms):
+            lo, hi = CHUNKS[c]
+            blocks = range((hi - lo) // P)
+            z = sb("z%d" % c, [P, (hi - lo) * PACK], BF16)
+            sums = [psum.tile([P, PACK, P], F32, name="sum%d_%d" % (c, b), tag="bank%d" % (4 + c + b)) for b in blocks]
+            for t in range(PACK):
+                for b in blocks:
+                    for term, opens in ((terms[0], True), (terms[1], False)):
+                        nc.tensor.matmul(
+                            sums[b][:, t, :],
+                            term[:, t, P * b : P * (b + 1)],
+                            identity[:],
+                            start=opens,
+                            stop=not opens,
+                            is_transpose=True,
+                        )
+            backs = []
+            for b in blocks:
+                turned = sb("turned%d_%d" % (c, b), [P, PACK * P], BF16)
+                nc.scalar.copy(
+                    turned[:].rearrange("j (u p e) -> j u p e", u=2, e=2),
+                    sums[b][:].rearrange("j (u e) p -> j u p e", u=2),
                 )
+                back = psum.tile([P, 2, P], F32, name="back%d_%d" % (c, b), tag="bank%d" % (6 + b))
+                for u in range(2):
+                    nc.tensor.transpose(back[:, u, :], turned[:].bitcast(F32)[:, P * u : P * (u + 1)], identity[:])
+                backs.append(back)
+            for b in blocks:
+                nc.scalar.copy(
+                    z[:].bitcast(F32)[:, 2 * P * b : 2 * P * (b + 1)].rearrange("p (j u) -> p j u", u=2),
+                    backs[b][:].rearrange("p u j -> p j u"),
+                )
+            return z
+
+        def sum_on_vector(c, terms):
+            lo, hi = CHUNKS[c]
+            z = sb("z%d" % c, [P, (hi - lo) * PACK], BF16, "z%d" % (c - 1))
+            nc.vector.tensor_tensor(
+                z[:].rearrange("p (c t) -> p c t", t=PACK),
+                terms[0][:].rearrange("p t c -> p c t"),
+                terms[1][:].rearrange("p t c -> p c t"),
+                ALU.add,
+            )
+            return z
+
+        def score(c, z):
+            lo, hi = CHUNKS[c]
+            n = hi - lo
             z_codes = sb("z_codes%d" % c, [P, n], U32)
             z_plane = sb("z_plane%d" % c, [P, n], U8)
             nc.vector.quantize_mx(out=z_codes[:].bitcast(FP8X4), scales=z_plane[:], in_=z[:])
-            own = sb("s_own%d" % c, [P, PACK, n], F32)
-            s_own.append(own)
             per_bank = 1 if c == last else S // n
-            first_bank = (0, 2, 3)[c]
+            tags = ((0, 1), (2,), (3, 4, 7, 5))[c]
             banks = [
-                psum.tile([P, per_bank, n], F32, name="s_bank%d_%d" % (c, g), tag="bank%d" % (first_bank + g))
-                for g in range(PACK // per_bank)
+                psum.tile([P, per_bank, n], F32, name="s_bank%d_%d" % (c, g), tag="bank%d" % tag)
+                for g, tag in enumerate(tags)
             ]
             for t in range(PACK):
                 rows = slice(P * t, P * (t + 1))
@@ -203,11 +227,18 @@ def tile_picked_pqcdotover_none_po_kernel(
                     stop=True,
                 )
             for t in range(PACK):
-                nc.scalar.activation(s_win[t][:, cols], banks[t // per_bank][:, t % per_bank, :], COPY, scale=0.0625)
+                nc.scalar.activation(s_win[t][:, lo:hi], banks[t // per_bank][:, t % per_bank, :], COPY, scale=0.0625)
             for g, bank in enumerate(banks):
                 nc.scalar.activation(
-                    own[:, per_bank * g : per_bank * (g + 1), :], bank[:], COPY, scale=0.75 * 0.0625
+                    s_own[c][:, per_bank * g : per_bank * (g + 1), :], bank[:], COPY, scale=0.75 * 0.0625
                 )
+
+        z_first = sum_on_tensor(0, products(0))
+        z_middle = sum_on_tensor(1, products(1))
+        score(0, z_first)
+        terms_last = products(2)
+        score(1, z_middle)
+        score(2, sum_on_vector(2, terms_last))
 
         out_rows = out_0.rearrange("(p t) j -> p t j", t=PACK)
         out_words = word_rows(out_1)

@@ -118,13 +118,15 @@ def tile_picked_pqcdotover_none_po_kernel(
             h_plain.append(plain)
             h_gated.append(gated)
 
-        c_codes_picked = pick("c_codes_picked", x_word_table, cand_t, U32, "staging")
         c_bytes_picked = pick("c_bytes_picked", x_byte_table, cand_t, U8, "d_word_table")
-        c_codes = deal_words("c_codes", c_codes_picked)
+        c_codes = sb("c_codes", [P, S], U32, "staging")
+        nc.vector.tensor_copy(
+            c_codes[:].rearrange("p (t m) -> p m t", t=PACK), x_word_table[:].indirect(cand_t[:])
+        )
         c_plane = deal_bytes("c_plane", c_bytes_picked)
 
         s_win = [sb("s_win%d" % t, [P, S], F32) for t in range(PACK)]
-        s_own = [sb("s_own%d" % c, [P, PACK, hi - lo], F32) for c, (lo, hi) in enumerate(CHUNKS)]
+        s_own = {}
         last = len(CHUNKS) - 1
 
         def products(c):
@@ -229,9 +231,10 @@ def tile_picked_pqcdotover_none_po_kernel(
             for t in range(PACK):
                 nc.scalar.activation(s_win[t][:, lo:hi], banks[t // per_bank][:, t % per_bank, :], COPY, scale=0.0625)
             for g, bank in enumerate(banks):
-                nc.scalar.activation(
-                    s_own[c][:, per_bank * g : per_bank * (g + 1), :], bank[:], COPY, scale=0.75 * 0.0625
-                )
+                own = sb("s_own%d_%d" % (c, g), [P, per_bank, n], F32)
+                nc.scalar.activation(own[:], bank[:], COPY, scale=0.75 * 0.0625)
+                for i in range(per_bank):
+                    s_own.setdefault((c, per_bank * g + i), own[:, i, :])
 
         z_first = sum_on_tensor(0, products(0))
         z_middle = sum_on_tensor(1, products(1))
@@ -243,32 +246,47 @@ def tile_picked_pqcdotover_none_po_kernel(
         out_rows = out_0.rearrange("(p t) j -> p t j", t=PACK)
         out_words = word_rows(out_1)
         y_plane = sb("y_plane", [P, S], U8)
-        for c, (lo, hi) in enumerate(CHUNKS):
-            n = hi - lo
-            cols = slice(lo, hi)
+
+        def fetch_both(c):
+            lo, hi = CHUNKS[c]
             ent = slice(lo // 16, hi // 16)
-            left = sb("left%d" % c, [P, PACK, n], F32)
-            right = sb("right%d" % c, [P, PACK, n], F32)
+            left = sb("left%d" % c, [P, PACK, hi - lo], F32)
+            right = sb("right%d" % c, [P, PACK, hi - lo], F32)
             for t in range(PACK):
-                nc.vector.tensor_tensor(
-                    left[:, t, :], s_win[t][:].indirect(n4_t[:, ent]), s_own[c][:, t, :], ALU.subtract
-                )
-                nc.vector.tensor_tensor(
-                    right[:, t, :], s_win[t][:].indirect(n5_t[:, ent]), s_own[c][:, t, :], ALU.subtract
-                )
-            y = sb("y%d" % c, [P, PACK, n], F32)
+                for side, entries in ((left, n4_t), (right, n5_t)):
+                    nc.vector.tensor_tensor(
+                        side[:, t, :], s_win[t][:].indirect(entries[:, ent]), s_own[c, t], ALU.subtract
+                    )
+            return left, right
+
+        def larger(c, left, right):
+            lo, hi = CHUNKS[c]
+            y = sb("y%d" % c, [P, PACK, hi - lo], F32)
             nc.vector.tensor_tensor(y[:], left[:], right[:], ALU.max)
-            nc.sync.dma_start(out_rows[:, :, cols], y[:])
-            y_round = sb("y_round%d" % c, [P, n, PACK], BF16)
-            regroup = nc.vector.tensor_copy if c == last else nc.scalar.copy
-            regroup(
-                y_round[:].rearrange("p (c i) t -> p c t i", i=4), y[:].rearrange("p t (c i) -> p c t i", i=4)
-            )
-            y_codes = sb("y_codes%d" % c, [P, n], U32)
+            nc.sync.dma_start(out_rows[:, :, lo:hi], y[:])
+            return y
+
+        def regroup(c, y, copy):
+            lo, hi = CHUNKS[c]
+            y_round = sb("y_round%d" % c, [P, hi - lo, PACK], BF16)
+            copy(y_round[:].rearrange("p (c i) t -> p c t i", i=4), y[:].rearrange("p t (c i) -> p c t i", i=4))
+            return y_round
+
+        def quantise(c, y_round, tag):
+            lo, hi = CHUNKS[c]
+            y_codes = sb("y_codes%d" % c, [P, hi - lo], U32, tag)
             nc.vector.quantize_mx(
-                out=y_codes[:].bitcast(FP8X4), scales=y_plane[:, cols], in_=y_round[:].rearrange("p c t -> p (c t)")
+                out=y_codes[:].bitcast(FP8X4), scales=y_plane[:, lo:hi], in_=y_round[:].rearrange("p c t -> p (c t)")
             )
-            nc.sync.dma_start(out_words[:, cols], y_codes[:].bitcast(I32))
+            nc.sync.dma_start(out_words[:, lo:hi], y_codes[:].bitcast(I32))
+
+        round_first = regroup(0, larger(0, *fetch_both(0)), nc.scalar.copy)
+        round_middle = regroup(1, larger(1, *fetch_both(1)), nc.scalar.copy)
+        sides_last = fetch_both(2)
+        quantise(0, round_first, "s_own2_2")
+        y_last = larger(2, *sides_last)
+        quantise(1, round_middle, "s_own2_3")
+        quantise(2, regroup(2, y_last, nc.vector.tensor_copy), None)
         for q in range(4):
             queue = nc.sync if q % 2 else nc.scalar
             queue.dma_start(

@@ -3,7 +3,7 @@ from contextlib import ExitStack
 import concourse.mybir as mybir
 from concourse.masks import make_identity
 
-K, T, S, G = 512, 1024, 512, 2048
+T, S, G = 1024, 512, 2048
 FLOPS = 2 * 2 * 512 * 512 * 512
 
 F32 = mybir.dt.float32
@@ -15,10 +15,18 @@ U8 = mybir.dt.uint8
 FP8X4 = mybir.dt.float8_e4m3fn_x4
 ALU = mybir.AluOpType
 COPY = mybir.ActivationFunctionType.Copy
+RELU = mybir.ActivationFunctionType.Relu
 
 P = 128
 PACK = 4
+QUADRANTS = 4
+LINE = 4
+PER_COLUMN = 16
 CHUNKS = ((0, 256), (256, 384), (384, 512))
+FIRST, MIDDLE, LAST = range(3)
+Z_SUM_BANK, Z_BACK_BANK = 4, 6
+S_BANKS = ((0, 1), (2,), (3, 4, 7, 5))
+Y_SUM_BANKS, Y_BACK_BANKS = (0, 1), (2, 6)
 
 
 def tile_picked_pqcdotover_none_po_kernel(
@@ -33,12 +41,16 @@ def tile_picked_pqcdotover_none_po_kernel(
             return keep.tile(shape, dtype, name=name, tag=tag or name, align_bytes=64)
 
         def load_list(name, src):
-            tile = sb(name, [P, S // 16], U16)
+            tile = sb(name, [P, S // PER_COLUMN], U16)
             nc.sync.dma_start(tile[:], src)
             return tile
 
         def word_rows(words):
             return words[0].rearrange("p c r -> p (c r)").bitcast(I32)
+
+        def entries_of(lists, c):
+            lo, hi = CHUNKS[c]
+            return lists[:, lo // PER_COLUMN : hi // PER_COLUMN]
 
         d_byte_table = sb("d_byte_table", [P, G], U8)
         x_byte_table = sb("x_byte_table", [P, T], U8)
@@ -59,7 +71,7 @@ def tile_picked_pqcdotover_none_po_kernel(
         n1_t = load_list("n1_t", n1)
         d_word_table = sb("d_word_table", [P, G], U32)
         nc.sync.dma_start(d_word_table[:].bitcast(I32), word_rows(d_words))
-        for q in range(4):
+        for q in range(QUADRANTS):
             nc.scalar.dma_start(
                 x_byte_table[32 * q : 32 * q + 4, :].bitcast(I32), x_scales[0][4 * q : 4 * q + 4, :].bitcast(I32)
             )
@@ -77,8 +89,8 @@ def tile_picked_pqcdotover_none_po_kernel(
         def deal_words(name, picked):
             dealt = sb(name, [P, S], U32)
             nc.vector.tensor_copy(
-                dealt[:].rearrange("p (t c i) -> p c t i", t=PACK, i=4),
-                picked[:].rearrange("p (c i t) -> p c t i", t=PACK, i=4),
+                dealt[:].rearrange("p (t c i) -> p c t i", t=PACK, i=LINE),
+                picked[:].rearrange("p (c i t) -> p c t i", t=PACK, i=LINE),
             )
             return dealt
 
@@ -91,7 +103,7 @@ def tile_picked_pqcdotover_none_po_kernel(
 
         x_codes = pick("x_codes", x_word_table, offs_t, U32)
         d_bytes = deal_bytes("d_bytes", pick("d_bytes_picked", d_byte_table, k1_t, U8, "staging"))
-        for q in range(4):
+        for q in range(QUADRANTS):
             nc.scalar.dma_start(
                 d_plane[32 * q : 32 * q + 4, :].bitcast(I32), d_bytes[32 * q : 32 * q + 32 : 8, :].bitcast(I32)
             )
@@ -127,30 +139,28 @@ def tile_picked_pqcdotover_none_po_kernel(
 
         s_win = [sb("s_win%d" % t, [P, S], F32) for t in range(PACK)]
         s_own = {}
-        last = len(CHUNKS) - 1
 
         def products(c):
             lo, hi = CHUNKS[c]
             n = hi - lo
-            ent = slice(lo // 16, hi // 16)
-            second = sb("second%d" % c, [P, PACK, n], F32, "z0" if c == last else "second")
-            first_prod = sb("first_prod", [P, PACK, n], F32) if c == 0 else second
+            second = sb("second%d" % c, [P, PACK, n], F32, "z%d" % FIRST if c == LAST else "second")
+            first_prod = sb("first_prod", [P, PACK, n], F32) if c == FIRST else second
             second_prod = sb("second_prod%d" % c, [P, PACK, n], F32)
 
             def fetch_second(t):
-                nc.vector.tensor_copy(second[:, t, :], h_gated[t][:].indirect(n2_t[:, ent]))
+                nc.vector.tensor_copy(second[:, t, :], h_gated[t][:].indirect(entries_of(n2_t, c)))
 
             def multiply_first(t):
                 nc.vector.tensor_tensor(
-                    first_prod[:, t, :], h_plain[t][:].indirect(n1_t[:, ent]), h_gated[t][:, lo:hi], ALU.mult
+                    first_prod[:, t, :], h_plain[t][:].indirect(entries_of(n1_t, c)), h_gated[t][:, lo:hi], ALU.mult
                 )
 
             def multiply_second(t):
                 nc.vector.tensor_tensor(
-                    second_prod[:, t, :], h_plain[t][:].indirect(n3_t[:, ent]), second[:, t, :], ALU.mult
+                    second_prod[:, t, :], h_plain[t][:].indirect(entries_of(n3_t, c)), second[:, t, :], ALU.mult
                 )
 
-            if c == 0:
+            if c == FIRST:
                 for t in range(PACK):
                     for step in (fetch_second, multiply_first, multiply_second):
                         step(t)
@@ -158,13 +168,16 @@ def tile_picked_pqcdotover_none_po_kernel(
                 for step in (fetch_second, multiply_second, multiply_first):
                     for t in range(PACK):
                         step(t)
-            return (first_prod, second_prod) if c == 0 else (second_prod, first_prod)
+            return (first_prod, second_prod) if c == FIRST else (second_prod, first_prod)
 
         def sum_on_tensor(c, terms):
             lo, hi = CHUNKS[c]
             blocks = range((hi - lo) // P)
             z = sb("z%d" % c, [P, (hi - lo) * PACK], BF16)
-            sums = [psum.tile([P, PACK, P], F32, name="sum%d_%d" % (c, b), tag="bank%d" % (4 + c + b)) for b in blocks]
+            sums = [
+                psum.tile([P, PACK, P], F32, name="sum%d_%d" % (c, b), tag="bank%d" % (Z_SUM_BANK + c + b))
+                for b in blocks
+            ]
             for t in range(PACK):
                 for b in blocks:
                     for term, opens in ((terms[0], True), (terms[1], False)):
@@ -183,7 +196,7 @@ def tile_picked_pqcdotover_none_po_kernel(
                     turned[:].rearrange("j (u p e) -> j u p e", u=2, e=2),
                     sums[b][:].rearrange("j (u e) p -> j u p e", u=2),
                 )
-                back = psum.tile([P, 2, P], F32, name="back%d_%d" % (c, b), tag="bank%d" % (6 + b))
+                back = psum.tile([P, 2, P], F32, name="back%d_%d" % (c, b), tag="bank%d" % (Z_BACK_BANK + b))
                 for u in range(2):
                     nc.tensor.transpose(back[:, u, :], turned[:].bitcast(F32)[:, P * u : P * (u + 1)], identity[:])
                 backs.append(back)
@@ -211,11 +224,10 @@ def tile_picked_pqcdotover_none_po_kernel(
             z_codes = sb("z_codes%d" % c, [P, n], U32)
             z_plane = sb("z_plane%d" % c, [P, n], U8)
             nc.vector.quantize_mx(out=z_codes[:].bitcast(FP8X4), scales=z_plane[:], in_=z[:])
-            per_bank = 1 if c == last else S // n
-            tags = ((0, 1), (2,), (3, 4, 7, 5))[c]
+            per_bank = PACK // len(S_BANKS[c])
             banks = [
-                psum.tile([P, per_bank, n], F32, name="s_bank%d_%d" % (c, g), tag="bank%d" % tag)
-                for g, tag in enumerate(tags)
+                psum.tile([P, per_bank, n], F32, name="s_bank%d_%d" % (c, g), tag="bank%d" % number)
+                for g, number in enumerate(S_BANKS[c])
             ]
             for t in range(PACK):
                 rows = slice(P * t, P * (t + 1))
@@ -230,18 +242,25 @@ def tile_picked_pqcdotover_none_po_kernel(
                 )
             for t in range(PACK):
                 nc.scalar.activation(s_win[t][:, lo:hi], banks[t // per_bank][:, t % per_bank, :], COPY, scale=0.0625)
+            return banks
+
+        def keep_own(c, banks, tag=None):
+            lo, hi = CHUNKS[c]
+            per_bank = PACK // len(banks)
             for g, bank in enumerate(banks):
-                own = sb("s_own%d_%d" % (c, g), [P, per_bank, n], F32)
-                nc.scalar.activation(own[:], bank[:], COPY, scale=0.75 * 0.0625)
+                own = sb("s_own%d_%d" % (c, g), [P, per_bank, hi - lo], F32, tag)
+                nc.scalar.activation(own[:], bank[:], COPY, scale=(-0.75 if c == FIRST else 0.75) * 0.0625)
                 for i in range(per_bank):
                     s_own.setdefault((c, per_bank * g + i), own[:, i, :])
 
-        z_first = sum_on_tensor(0, products(0))
-        z_middle = sum_on_tensor(1, products(1))
-        score(0, z_first)
-        terms_last = products(2)
-        score(1, z_middle)
-        score(2, sum_on_vector(2, terms_last))
+        z_first = sum_on_tensor(FIRST, products(FIRST))
+        z_middle = sum_on_tensor(MIDDLE, products(MIDDLE))
+        keep_own(FIRST, score(FIRST, z_first))
+        terms_last = products(LAST)
+        banks_middle = score(MIDDLE, z_middle)
+        banks_last = score(LAST, sum_on_vector(LAST, terms_last))
+        keep_own(MIDDLE, banks_middle, "z_codes%d" % LAST)
+        keep_own(LAST, banks_last)
 
         out_rows = out_0.rearrange("(p t) j -> p t j", t=PACK)
         out_words = word_rows(out_1)
@@ -249,45 +268,89 @@ def tile_picked_pqcdotover_none_po_kernel(
 
         def fetch_both(c):
             lo, hi = CHUNKS[c]
-            ent = slice(lo // 16, hi // 16)
-            left = sb("left%d" % c, [P, PACK, hi - lo], F32)
-            right = sb("right%d" % c, [P, PACK, hi - lo], F32)
+            sides = sb("sides%d" % c, [P, 2, PACK, hi - lo], F32)
+            left, right = sides[:, 0], sides[:, 1]
             for t in range(PACK):
-                for side, entries in ((left, n4_t), (right, n5_t)):
+                for side, lists in ((left, n4_t), (right, n5_t)):
                     nc.vector.tensor_tensor(
-                        side[:, t, :], s_win[t][:].indirect(entries[:, ent]), s_own[c, t], ALU.subtract
+                        side[:, t, :], s_win[t][:].indirect(entries_of(lists, c)), s_own[c, t], ALU.subtract
                     )
             return left, right
 
         def larger(c, left, right):
             lo, hi = CHUNKS[c]
             y = sb("y%d" % c, [P, PACK, hi - lo], F32)
-            nc.vector.tensor_tensor(y[:], left[:], right[:], ALU.max)
+            nc.vector.tensor_tensor(y[:], left, right, ALU.max)
             nc.sync.dma_start(out_rows[:, :, lo:hi], y[:])
             return y
 
-        def regroup(c, y, copy):
+        def regroup(c, y, copy, tag=None):
             lo, hi = CHUNKS[c]
-            y_round = sb("y_round%d" % c, [P, hi - lo, PACK], BF16)
-            copy(y_round[:].rearrange("p (c i) t -> p c t i", i=4), y[:].rearrange("p t (c i) -> p c t i", i=4))
+            y_round = sb("y_round%d" % c, [P, hi - lo, PACK], BF16, tag)
+            copy(y_round[:].rearrange("p (c i) t -> p c t i", i=LINE), y[:].rearrange("p t (c i) -> p c t i", i=LINE))
             return y_round
 
-        def quantise(c, y_round, tag):
+        def quantise(c, y_round, y_codes):
             lo, hi = CHUNKS[c]
-            y_codes = sb("y_codes%d" % c, [P, hi - lo], U32, tag)
             nc.vector.quantize_mx(
-                out=y_codes[:].bitcast(FP8X4), scales=y_plane[:, lo:hi], in_=y_round[:].rearrange("p c t -> p (c t)")
+                out=y_codes.bitcast(FP8X4), scales=y_plane[:, lo:hi], in_=y_round[:].rearrange("p c t -> p (c t)")
             )
-            nc.sync.dma_start(out_words[:, lo:hi], y_codes[:].bitcast(I32))
 
-        round_first = regroup(0, larger(0, *fetch_both(0)), nc.scalar.copy)
-        round_middle = regroup(1, larger(1, *fetch_both(1)), nc.scalar.copy)
-        sides_last = fetch_both(2)
-        quantise(0, round_first, "s_own2_2")
-        y_last = larger(2, *sides_last)
-        quantise(1, round_middle, "s_own2_3")
-        quantise(2, regroup(2, y_last, nc.vector.tensor_copy), None)
-        for q in range(4):
+        def larger_on_tensor(c):
+            lo, hi = CHUNKS[c]
+            n = hi - lo
+            blocks = range(n // P)
+            at_n5 = sb("at_n5", [P, PACK, n], F32)
+            excess = sb("excess", [P, PACK, n], F32)
+            gain = sb("gain", [P, PACK, n], F32)
+            sums = [psum.tile([P, PACK, P], F32, name="y_sum%d" % b, tag="bank%d" % Y_SUM_BANKS[b]) for b in blocks]
+            for t in range(PACK):
+                nc.vector.tensor_copy(at_n5[:, t, :], s_win[t][:].indirect(entries_of(n5_t, c)))
+            for t in range(PACK):
+                nc.vector.tensor_tensor(
+                    excess[:, t, :], s_win[t][:].indirect(entries_of(n4_t, c)), at_n5[:, t, :], ALU.subtract
+                )
+                nc.scalar.activation(gain[:, t, :], excess[:, t, :], RELU)
+                terms = (at_n5[:, t, :], s_own[c, t], gain[:, t, :])
+                for i, term in enumerate(terms):
+                    for b in blocks:
+                        nc.tensor.matmul(
+                            sums[b][:, t, :],
+                            term[:, P * b : P * (b + 1)],
+                            identity[:],
+                            start=i == 0,
+                            stop=i == len(terms) - 1,
+                            is_transpose=True,
+                        )
+            y = sb("y%d" % c, [P, PACK, n], F32)
+            y_round = sb("y_round%d" % c, [P, n, PACK], BF16)
+            backs = []
+            for b in blocks:
+                turned = sb("y_turned%d" % b, [P, PACK, P], F32)
+                nc.scalar.copy(turned[:], sums[b][:])
+                back = psum.tile([P, PACK, P], F32, name="y_back%d" % b, tag="bank%d" % Y_BACK_BANKS[b])
+                for t in range(PACK):
+                    nc.tensor.transpose(back[:, t, :], turned[:, t, :], identity[:])
+                backs.append(back)
+            for b in blocks:
+                nc.scalar.copy(y_round[:, P * b : P * (b + 1), :], backs[b][:].rearrange("p t c -> p c t"))
+                nc.scalar.copy(y[:, :, P * b : P * (b + 1)], backs[b][:])
+            nc.scalar.dma_start(out_rows[:, :, lo:hi], y[:])
+            return y_round
+
+        round_first = larger_on_tensor(FIRST)
+        round_middle = regroup(MIDDLE, larger(MIDDLE, *fetch_both(MIDDLE)), nc.scalar.copy, "y_turned1")
+        sides_last = fetch_both(LAST)
+        split = CHUNKS[LAST][0]
+        codes_early = sb("y_codes_early", [P, split], U32, "s_own%d_%d" % (LAST, PACK - 2))
+        quantise(FIRST, round_first, codes_early[:, : CHUNKS[FIRST][1]])
+        y_last = larger(LAST, *sides_last)
+        quantise(MIDDLE, round_middle, codes_early[:, CHUNKS[MIDDLE][0] :])
+        nc.sync.dma_start(out_words[:, :split], codes_early[:].bitcast(I32))
+        codes_last = sb("y_codes_last", [P, S - split], U32)
+        quantise(LAST, regroup(LAST, y_last, nc.vector.tensor_copy), codes_last[:])
+        nc.sync.dma_start(out_words[:, split:], codes_last[:].bitcast(I32))
+        for q in range(QUADRANTS):
             queue = nc.sync if q % 2 else nc.scalar
             queue.dma_start(
                 out_2[0][4 * q : 4 * q + 4, :].bitcast(I32), y_plane[32 * q : 32 * q + 4, :].bitcast(I32)

from contextlib import ExitStack

import concourse.mybir as mybir
from concourse.masks import make_identity

T, S, G = 1024, 512, 2048
FLOPS = 2 * 2 * 512 * 512 * 512

F32 = mybir.dt.float32
BF16 = mybir.dt.bfloat16
I32 = mybir.dt.int32
U32 = mybir.dt.uint32
U16 = mybir.dt.uint16
U8 = mybir.dt.uint8
FP8X4 = mybir.dt.float8_e4m3fn_x4
ALU = mybir.AluOpType
COPY = mybir.ActivationFunctionType.Copy
RELU = mybir.ActivationFunctionType.Relu

P = 128
PACK = 4
QUADRANTS = 4
LINE = 4
PER_COLUMN = 16
CHUNKS = ((0, 256), (256, 384), (384, 512))
FIRST, MIDDLE, LAST = range(3)
Z_SUM_BANK, Z_BACK_BANK = 4, 6
S_BANKS = ((0, 1), (2,), (3, 4, 7, 5))
Y_SUM_BANKS, Y_BACK_BANKS = (0, 1), (2, 6)


def tile_picked_pqcdotover_none_po_kernel(
    tc, x_words, x_scales, d_words, d_scales, gs, offs, k1, n1, n2, n3, cand, n4, n5, out_0, out_1, out_2
):
    nc = tc.nc
    with ExitStack() as ctx:
        keep = ctx.enter_context(tc.tile_pool(name="keep", bufs=1))
        psum = ctx.enter_context(tc.psum_pool(name="psum", bufs=1))

        def sb(name, shape, dtype, tag=None):
            return keep.tile(shape, dtype, name=name, tag=tag or name, align_bytes=64)

        def load_list(name, src):
            tile = sb(name, [P, S // PER_COLUMN], U16)
            nc.sync.dma_start(tile[:], src)
            return tile

        def word_rows(words):
            return words[0].rearrange("p c r -> p (c r)").bitcast(I32)

        def entries_of(lists, c):
            lo, hi = CHUNKS[c]
            return lists[:, lo // PER_COLUMN : hi // PER_COLUMN]

        d_byte_table = sb("d_byte_table", [P, G], U8)
        x_byte_table = sb("x_byte_table", [P, T], U8)
        d_plane = sb("d_plane", [P, S], U8)
        nc.gpsimd.memset(d_byte_table[:].bitcast(I32), 0)
        nc.vector.memset(x_byte_table[:].bitcast(I32), 0)
        nc.vector.memset(d_plane[:].bitcast(I32), 0)
        identity = sb("identity", [P, P], F32)
        make_identity(nc, identity[:])

        x_word_table = sb("x_word_table", [P, T], U32)
        nc.sync.dma_start(x_word_table[:].bitcast(I32), word_rows(x_words))
        offs_t = load_list("offs_t", offs)
        k1_t = load_list("k1_t", k1)
        nc.sync.dma_start(d_byte_table[0:P:8, :].bitcast(I32), d_scales[0].bitcast(I32))
        cand_t = load_list("cand_t", cand)
        n2_t = load_list("n2_t", n2)
        n1_t = load_list("n1_t", n1)
        d_word_table = sb("d_word_table", [P, G], U32)
        nc.sync.dma_start(d_word_table[:].bitcast(I32), word_rows(d_words))
        for q in range(QUADRANTS):
            nc.scalar.dma_start(
                x_byte_table[32 * q : 32 * q + 4, :].bitcast(I32), x_scales[0][4 * q : 4 * q + 4, :].bitcast(I32)
            )
        gs_t = sb("gs_t", [P, PACK], F32)
        nc.gpsimd.dma_start(gs_t[:], gs.rearrange("(p t) o -> p (t o)", t=PACK))
        n3_t = load_list("n3_t", n3)
        n4_t = load_list("n4_t", n4)
        n5_t = load_list("n5_t", n5)

        def pick(name, table, entries, dtype, tag=None):
            picked = sb(name, [P, S], dtype, tag)
            nc.vector.tensor_copy(picked[:], table[:].indirect(entries[:]))
            return picked

        def deal_words(name, picked):
            dealt = sb(name, [P, S], U32)
            nc.vector.tensor_copy(
                dealt[:].rearrange("p (t c i) -> p c t i", t=PACK, i=LINE),
                picked[:].rearrange("p (c i t) -> p c t i", t=PACK, i=LINE),
            )
            return dealt

        def deal_bytes(name, picked):
            dealt = sb(name, [P, S], U8)
            nc.vector.tensor_copy(
                dealt[:].rearrange("p (t m) -> p t m", t=PACK), picked[:].rearrange("p (m t) -> p t m", t=PACK)
            )
            return dealt

        x_codes = pick("x_codes", x_word_table, offs_t, U32)
        d_bytes = deal_bytes("d_bytes", pick("d_bytes_picked", d_byte_table, k1_t, U8, "staging"))
        for q in range(QUADRANTS):
            nc.scalar.dma_start(
                d_plane[32 * q : 32 * q + 4, :].bitcast(I32), d_bytes[32 * q : 32 * q + 32 : 8, :].bitcast(I32)
            )
        d_codes = deal_words("d_codes", pick("d_codes_picked", d_word_table, k1_t, U32, "staging"))
        x_plane = pick("x_plane", x_byte_table, offs_t, U8)

        h_plain, h_gated = [], []
        for t in range(PACK):
            rows = slice(P * t, P * (t + 1))
            bank = psum.tile([P, S], F32, name="h_bank%d" % t, tag="bank%d" % t)
            nc.tensor.matmul_mx(
                out=bank[:],
                lhsT=d_codes[:, rows].bitcast(FP8X4),
                lhsT_scale=d_plane[:, rows],
                rhs=x_codes[:].bitcast(FP8X4),
                rhs_scale=x_plane[:],
                start=True,
                stop=True,
            )
            gated = sb("h_gated%d" % t, [P, S], F32)
            nc.scalar.activation(gated[:], bank[:], COPY, scale=gs_t[:, t : t + 1])
            plain = sb("h_plain%d" % t, [P, S], F32)
            nc.scalar.activation(plain[:], bank[:], COPY, scale=0.75 * 0.0625 * 0.0625)
            h_plain.append(plain)
            h_gated.append(gated)

        c_bytes_picked = pick("c_bytes_picked", x_byte_table, cand_t, U8, "d_word_table")
        c_codes = sb("c_codes", [P, S], U32, "staging")
        nc.vector.tensor_copy(
            c_codes[:].rearrange("p (t m) -> p m t", t=PACK), x_word_table[:].indirect(cand_t[:])
        )
        c_plane = deal_bytes("c_plane", c_bytes_picked)

        s_win = [sb("s_win%d" % t, [P, S], F32) for t in range(PACK)]
        s_own = {}

        def products(c):
            lo, hi = CHUNKS[c]
            n = hi - lo
            second = sb("second%d" % c, [P, PACK, n], F32, "z%d" % FIRST if c == LAST else "second")
            first_prod = sb("first_prod", [P, PACK, n], F32) if c == FIRST else second
            second_prod = sb("second_prod%d" % c, [P, PACK, n], F32)

            def fetch_second(t):
                nc.vector.tensor_copy(second[:, t, :], h_gated[t][:].indirect(entries_of(n2_t, c)))

            def multiply_first(t):
                nc.vector.tensor_tensor(
                    first_prod[:, t, :], h_plain[t][:].indirect(entries_of(n1_t, c)), h_gated[t][:, lo:hi], ALU.mult
                )

            def multiply_second(t):
                nc.vector.tensor_tensor(
                    second_prod[:, t, :], h_plain[t][:].indirect(entries_of(n3_t, c)), second[:, t, :], ALU.mult
                )

            if c == FIRST:
                for t in range(PACK):
                    for step in (fetch_second, multiply_first, multiply_second):
                        step(t)
            else:
                for step in (fetch_second, multiply_second, multiply_first):
                    for t in range(PACK):
                        step(t)
            return (first_prod, second_prod) if c == FIRST else (second_prod, first_prod)

        def sum_on_tensor(c, terms):
            lo, hi = CHUNKS[c]
            blocks = range((hi - lo) // P)
            z = sb("z%d" % c, [P, (hi - lo) * PACK], BF16)
            sums = [
                psum.tile([P, PACK, P], F32, name="sum%d_%d" % (c, b), tag="bank%d" % (Z_SUM_BANK + c + b))
                for b in blocks
            ]
            for t in range(PACK):
                for b in blocks:
                    for term, opens in ((terms[0], True), (terms[1], False)):
                        nc.tensor.matmul(
                            sums[b][:, t, :],
                            term[:, t, P * b : P * (b + 1)],
                            identity[:],
                            start=opens,
                            stop=not opens,
                            is_transpose=True,
                        )
            backs = []
            for b in blocks:
                turned = sb("turned%d_%d" % (c, b), [P, PACK * P], BF16)
                nc.scalar.copy(
                    turned[:].rearrange("j (u p e) -> j u p e", u=2, e=2),
                    sums[b][:].rearrange("j (u e) p -> j u p e", u=2),
                )
                back = psum.tile([P, 2, P], F32, name="back%d_%d" % (c, b), tag="bank%d" % (Z_BACK_BANK + b))
                for u in range(2):
                    nc.tensor.transpose(back[:, u, :], turned[:].bitcast(F32)[:, P * u : P * (u + 1)], identity[:])
                backs.append(back)
            for b in blocks:
                nc.scalar.copy(
                    z[:].bitcast(F32)[:, 2 * P * b : 2 * P * (b + 1)].rearrange("p (j u) -> p j u", u=2),
                    backs[b][:].rearrange("p u j -> p j u"),
                )
            return z

        def sum_on_vector(c, terms):
            lo, hi = CHUNKS[c]
            z = sb("z%d" % c, [P, (hi - lo) * PACK], BF16, "z%d" % (c - 1))
            nc.vector.tensor_tensor(
                z[:].rearrange("p (c t) -> p c t", t=PACK),
                terms[0][:].rearrange("p t c -> p c t"),
                terms[1][:].rearrange("p t c -> p c t"),
                ALU.add,
            )
            return z

        def score(c, z):
            lo, hi = CHUNKS[c]
            n = hi - lo
            z_codes = sb("z_codes%d" % c, [P, n], U32)
            z_plane = sb("z_plane%d" % c, [P, n], U8)
            nc.vector.quantize_mx(out=z_codes[:].bitcast(FP8X4), scales=z_plane[:], in_=z[:])
            per_bank = PACK // len(S_BANKS[c])
            banks = [
                psum.tile([P, per_bank, n], F32, name="s_bank%d_%d" % (c, g), tag="bank%d" % number)
                for g, number in enumerate(S_BANKS[c])
            ]
            for t in range(PACK):
                rows = slice(P * t, P * (t + 1))
                nc.tensor.matmul_mx(
                    out=banks[t // per_bank][:, t % per_bank, :],
                    lhsT=c_codes[:, rows].bitcast(FP8X4),
                    lhsT_scale=c_plane[:, rows],
                    rhs=z_codes[:].bitcast(FP8X4),
                    rhs_scale=z_plane[:],
                    start=True,
                    stop=True,
                )
            for t in range(PACK):
                nc.scalar.activation(s_win[t][:, lo:hi], banks[t // per_bank][:, t % per_bank, :], COPY, scale=0.0625)
            return banks

        def keep_own(c, banks, tag=None):
            lo, hi = CHUNKS[c]
            per_bank = PACK // len(banks)
            for g, bank in enumerate(banks):
                own = sb("s_own%d_%d" % (c, g), [P, per_bank, hi - lo], F32, tag)
                nc.scalar.activation(own[:], bank[:], COPY, scale=(-0.75 if c == FIRST else 0.75) * 0.0625)
                for i in range(per_bank):
                    s_own.setdefault((c, per_bank * g + i), own[:, i, :])

        z_first = sum_on_tensor(FIRST, products(FIRST))
        z_middle = sum_on_tensor(MIDDLE, products(MIDDLE))
        keep_own(FIRST, score(FIRST, z_first))
        terms_last = products(LAST)
        banks_middle = score(MIDDLE, z_middle)
        banks_last = score(LAST, sum_on_vector(LAST, terms_last))
        keep_own(MIDDLE, banks_middle, "z_codes%d" % LAST)
        keep_own(LAST, banks_last)

        out_rows = out_0.rearrange("(p t) j -> p t j", t=PACK)
        out_words = word_rows(out_1)
        y_plane = sb("y_plane", [P, S], U8)

        def fetch_both(c):
            lo, hi = CHUNKS[c]
            sides = sb("sides%d" % c, [P, 2, PACK, hi - lo], F32)
            left, right = sides[:, 0], sides[:, 1]
            for t in range(PACK):
                for side, lists in ((left, n4_t), (right, n5_t)):
                    nc.vector.tensor_tensor(
                        side[:, t, :], s_win[t][:].indirect(entries_of(lists, c)), s_own[c, t], ALU.subtract
                    )
            return left, right

        def larger(c, left, right):
            lo, hi = CHUNKS[c]
            y = sb("y%d" % c, [P, PACK, hi - lo], F32)
            nc.vector.tensor_tensor(y[:], left, right, ALU.max)
            nc.sync.dma_start(out_rows[:, :, lo:hi], y[:])
            return y

        def regroup(c, y, copy, tag=None):
            lo, hi = CHUNKS[c]
            y_round = sb("y_round%d" % c, [P, hi - lo, PACK], BF16, tag)
            copy(y_round[:].rearrange("p (c i) t -> p c t i", i=LINE), y[:].rearrange("p t (c i) -> p c t i", i=LINE))
            return y_round

        def quantise(c, y_round, y_codes):
            lo, hi = CHUNKS[c]
            nc.vector.quantize_mx(
                out=y_codes.bitcast(FP8X4), scales=y_plane[:, lo:hi], in_=y_round[:].rearrange("p c t -> p (c t)")
            )

        def larger_on_tensor(c):
            lo, hi = CHUNKS[c]
            n = hi - lo
            blocks = range(n // P)
            at_n5 = sb("at_n5", [P, PACK, n], F32)
            excess = sb("excess", [P, PACK, n], F32)
            gain = sb("gain", [P, PACK, n], F32)
            sums = [psum.tile([P, PACK, P], F32, name="y_sum%d" % b, tag="bank%d" % Y_SUM_BANKS[b]) for b in blocks]
            for t in range(PACK):
                nc.vector.tensor_copy(at_n5[:, t, :], s_win[t][:].indirect(entries_of(n5_t, c)))
            for t in range(PACK):
                nc.vector.tensor_tensor(
                    excess[:, t, :], s_win[t][:].indirect(entries_of(n4_t, c)), at_n5[:, t, :], ALU.subtract
                )
                nc.scalar.activation(gain[:, t, :], excess[:, t, :], RELU)
                terms = (at_n5[:, t, :], s_own[c, t], gain[:, t, :])
                for i, term in enumerate(terms):
                    for b in blocks:
                        nc.tensor.matmul(
                            sums[b][:, t, :],
                            term[:, P * b : P * (b + 1)],
                            identity[:],
                            start=i == 0,
                            stop=i == len(terms) - 1,
                            is_transpose=True,
                        )
            y = sb("y%d" % c, [P, PACK, n], F32)
            y_round = sb("y_round%d" % c, [P, n, PACK], BF16)
            backs = []
            for b in blocks:
                turned = sb("y_turned%d" % b, [P, PACK, P], F32)
                nc.scalar.copy(turned[:], sums[b][:])
                back = psum.tile([P, PACK, P], F32, name="y_back%d" % b, tag="bank%d" % Y_BACK_BANKS[b])
                for t in range(PACK):
                    nc.tensor.transpose(back[:, t, :], turned[:, t, :], identity[:])
                backs.append(back)
            for b in blocks:
                nc.scalar.copy(y_round[:, P * b : P * (b + 1), :], backs[b][:].rearrange("p t c -> p c t"))
                nc.scalar.copy(y[:, :, P * b : P * (b + 1)], backs[b][:])
            nc.scalar.dma_start(out_rows[:, :, lo:hi], y[:])
            return y_round

        round_first = larger_on_tensor(FIRST)
        round_middle = regroup(MIDDLE, larger(MIDDLE, *fetch_both(MIDDLE)), nc.scalar.copy, "y_turned1")
        sides_last = fetch_both(LAST)
        split = CHUNKS[LAST][0]
        codes_early = sb("y_codes_early", [P, split], U32, "s_own%d_%d" % (LAST, PACK - 2))
        quantise(FIRST, round_first, codes_early[:, : CHUNKS[FIRST][1]])
        y_last = larger(LAST, *sides_last)
        quantise(MIDDLE, round_middle, codes_early[:, CHUNKS[MIDDLE][0] :])
        nc.sync.dma_start(out_words[:, :split], codes_early[:].bitcast(I32))
        codes_last = sb("y_codes_last", [P, S - split], U32)
        quantise(LAST, regroup(LAST, y_last, nc.vector.tensor_copy), codes_last[:])
        nc.sync.dma_start(out_words[:, split:], codes_last[:].bitcast(I32))
        for q in range(QUADRANTS):
            queue = nc.sync if q % 2 else nc.scalar
            queue.dma_start(
                out_2[0][4 * q : 4 * q + 4, :].bitcast(I32), y_plane[32 * q : 32 * q + 4, :].bitcast(I32)
            )
